import numpy as np
import ml_dtypes

BF16 = ml_dtypes.bfloat16


def bf(x):
    return np.asarray(x, np.float32).astype(BF16)


def f32(x):
    return np.asarray(x, np.float32)


def f64(x):
    return np.asarray(x).astype(np.float64)


def striped(idx):
    return np.tile(idx.reshape(-1, 16).T, (8, 1))


S, K, M, N, E, Q, O = 256, 256, 384, 128, 2, 64, 128


def setup_inputs():
    return {"base": bf(np.random.standard_normal((M, S))), "x": bf(np.random.standard_normal((K, N))), "w": bf(1.2 * np.random.standard_normal((E, K, M)) / np.sqrt(K)), "w2": bf(np.random.standard_normal((M, O)) / np.sqrt(2 * M)), "b": f32(0.5 * np.random.standard_normal((O, 1))), "offs": striped(np.random.permutation(S)[:N])}


def reference(base, x, w, w2, b, offs):
    idx = offs[:16].T.reshape(-1)
    z = f64(base).copy()
    for e in range(E):
        z[:, idx[e * Q : (e + 1) * Q]] += f64(w)[e].T @ f64(x)[:, e * Q : (e + 1) * Q]
    y = f64(w2).T @ z
    return np.maximum(y + f64(b), 0.0)

@@ -1,0 +1,64 @@
+import concourse.mybir as mybir
+from concourse.masks import make_identity
+
+P = 128
+S, K, M, N, E, O = 256, 256, 384, 128, 2, 128
+Q = N // E
+KB = K // P
+MB = M // P
+Q_COLS = Q // 16
+BF16, F32, U16 = mybir.dt.bfloat16, mybir.dt.float32, mybir.dt.uint16
+ADD, MAX = mybir.AluOpType.add, mybir.AluOpType.max
+
+FLOPS = 2 * K * N * M + 2 * M * S * O
+
+
+def tile_rows_thenproj_relu_kernel(tc, base, x, w, w2, b, offs, out):
+    nc = tc.nc
+    with (
+        tc.tile_pool(name="held", bufs=1) as held,
+        tc.psum_pool(name="psum", bufs=1) as psum,
+    ):
+        base_sb = held.tile([P, MB, S], BF16, name="base_sb")
+        offsets = held.tile([P, N // 16], U16, name="offsets")
+        x_sb = held.tile([P, KB, N], BF16, name="x_sb")
+        w_sb = held.tile([P, E, KB, M], BF16, name="w_sb")
+        w2_sb = held.tile([P, MB, O], BF16, name="w2_sb")
+        b_sb = held.tile([P, 1], F32, name="b_sb")
+
+        nc.sync.dma_start(base_sb[:], base.rearrange("(a p) s -> p a s", p=P))
+        nc.sync.dma_start(offsets[:], offs)
+        nc.sync.dma_start(x_sb[:], x.rearrange("(p c) n -> p c n", c=KB))
+        for e in range(E):
+            nc.sync.dma_start(w_sb[:, e], w[e].rearrange("(p c) m -> p c m", c=KB))
+        nc.sync.dma_start(w2_sb[:], w2.rearrange("(a p) o -> p a o", p=P))
+        nc.sync.dma_start(b_sb[:], b)
+
+        identity = held.tile([P, P], BF16, name="identity")
+        make_identity(nc, identity[:])
+
+        windows = [psum.tile([P, S], F32, name=f"window{a}") for a in range(MB)]
+        for a in range(MB):
+            nc.tensor.matmul(windows[a][:], identity[:], base_sb[:, a], start=True, stop=False)
+
+        for a in range(MB):
+            for e in range(E):
+                places = offsets[:, e * Q_COLS : (e + 1) * Q_COLS]
+                for c in range(KB):
+                    nc.tensor.matmul(
+                        windows[a][:].indirect(places),
+                        w_sb[:, e, c, a * P : (a + 1) * P],
+                        x_sb[:, c, e * Q : (e + 1) * Q],
+                        start=False,
+                        stop=(e == E - 1 and c == KB - 1),
+                    )
+
+        y = psum.tile([P, S], F32, name="y")
+        for a in range(MB):
+            z = held.tile([P, S], BF16, name=f"z{a}")
+            nc.vector.tensor_copy(z[:], windows[a][:])
+            nc.tensor.matmul(y[:], w2_sb[:, a], z[:], start=(a == 0), stop=(a == MB - 1))
+
+        result = held.tile([P, S], F32, name="result")
+        nc.vector.tensor_scalar(result[:], y[:], b_sb[:], 0.0, ADD, MAX)
+        nc.sync.dma_start(out, result[:])

@@ -9,6 +9,7 @@ MB = M // P
 Q_COLS = Q // 16
 BF16, F32, U16 = mybir.dt.bfloat16, mybir.dt.float32, mybir.dt.uint16
 ADD, MAX = mybir.AluOpType.add, mybir.AluOpType.max
+WARM_UPS, WARM_COLS = 5, 512
 
 FLOPS = 2 * K * N * M + 2 * M * S * O
 
@@ -33,6 +34,12 @@ def tile_rows_thenproj_relu_kernel(tc, base, x, w, w2, b, offs, out):
             nc.sync.dma_start(w_sb[:, e], w[e].rearrange("(p c) m -> p c m", c=KB))
         nc.sync.dma_start(w2_sb[:], w2.rearrange("(a p) o -> p a o", p=P))
         nc.sync.dma_start(b_sb[:], b)
+
+        zeros = held.tile([P, WARM_COLS], BF16, name="zeros")
+        nc.vector.memset(zeros[:], 0.0)
+        spare = psum.tile([P, WARM_COLS], F32, name="spare")
+        for i in range(WARM_UPS):
+            nc.tensor.matmul(spare[:], zeros[:, :P], zeros[:], start=True, stop=True)
 
         identity = held.tile([P, P], BF16, name="identity")
         make_identity(nc, identity[:])

@@ -9,7 +9,7 @@ MB = M // P
 Q_COLS = Q // 16
 BF16, F32, U16 = mybir.dt.bfloat16, mybir.dt.float32, mybir.dt.uint16
 ADD, MAX = mybir.AluOpType.add, mybir.AluOpType.max
-WARM_UPS, WARM_COLS = 5, 512
+WARM_UPS, WARM_COLS = 3, 512
 
 FLOPS = 2 * K * N * M + 2 * M * S * O
 

import concourse.mybir as mybir
from concourse.masks import make_identity

P = 128
S, K, M, N, E, O = 256, 256, 384, 128, 2, 128
Q = N // E
KB = K // P
MB = M // P
Q_COLS = Q // 16
BF16, F32, U16 = mybir.dt.bfloat16, mybir.dt.float32, mybir.dt.uint16
ADD, MAX = mybir.AluOpType.add, mybir.AluOpType.max
WARM_UPS, WARM_COLS = 3, 512

FLOPS = 2 * K * N * M + 2 * M * S * O


def tile_rows_thenproj_relu_kernel(tc, base, x, w, w2, b, offs, out):
    nc = tc.nc
    with (
        tc.tile_pool(name="held", bufs=1) as held,
        tc.psum_pool(name="psum", bufs=1) as psum,
    ):
        base_sb = held.tile([P, MB, S], BF16, name="base_sb")
        offsets = held.tile([P, N // 16], U16, name="offsets")
        x_sb = held.tile([P, KB, N], BF16, name="x_sb")
        w_sb = held.tile([P, E, KB, M], BF16, name="w_sb")
        w2_sb = held.tile([P, MB, O], BF16, name="w2_sb")
        b_sb = held.tile([P, 1], F32, name="b_sb")

        nc.sync.dma_start(base_sb[:], base.rearrange("(a p) s -> p a s", p=P))
        nc.sync.dma_start(offsets[:], offs)
        nc.sync.dma_start(x_sb[:], x.rearrange("(p c) n -> p c n", c=KB))
        for e in range(E):
            nc.sync.dma_start(w_sb[:, e], w[e].rearrange("(p c) m -> p c m", c=KB))
        nc.sync.dma_start(w2_sb[:], w2.rearrange("(a p) o -> p a o", p=P))
        nc.sync.dma_start(b_sb[:], b)

        zeros = held.tile([P, WARM_COLS], BF16, name="zeros")
        nc.vector.memset(zeros[:], 0.0)
        spare = psum.tile([P, WARM_COLS], F32, name="spare")
        for i in range(WARM_UPS):
            nc.tensor.matmul(spare[:], zeros[:, :P], zeros[:], start=True, stop=True)

        identity = held.tile([P, P], BF16, name="identity")
        make_identity(nc, identity[:])

        windows = [psum.tile([P, S], F32, name=f"window{a}") for a in range(MB)]
        for a in range(MB):
            nc.tensor.matmul(windows[a][:], identity[:], base_sb[:, a], start=True, stop=False)

        for a in range(MB):
            for e in range(E):
                places = offsets[:, e * Q_COLS : (e + 1) * Q_COLS]
                for c in range(KB):
                    nc.tensor.matmul(
                        windows[a][:].indirect(places),
                        w_sb[:, e, c, a * P : (a + 1) * P],
                        x_sb[:, c, e * Q : (e + 1) * Q],
                        start=False,
                        stop=(e == E - 1 and c == KB - 1),
                    )

        y = psum.tile([P, S], F32, name="y")
        for a in range(MB):
            z = held.tile([P, S], BF16, name=f"z{a}")
            nc.vector.tensor_copy(z[:], windows[a][:])
            nc.tensor.matmul(y[:], w2_sb[:, a], z[:], start=(a == 0), stop=(a == MB - 1))

        result = held.tile([P, S], F32, name="result")
        nc.vector.tensor_scalar(result[:], y[:], b_sb[:], 0.0, ADD, MAX)
        nc.sync.dma_start(out, result[:])
